import numpy as np
import ml_dtypes


def mxq(x, axis, fmt="e4m3"):
    dtype, down = {"e4m3": (ml_dtypes.float8_e4m3fn, 7), "e5m2": (ml_dtypes.float8_e5m2, 14)}[fmt]
    v = np.moveaxis(np.asarray(x, np.float32).astype(ml_dtypes.bfloat16).astype(np.float64), axis, -1)
    blocks = v.reshape(v.shape[:-1] + (-1, 32))
    amax = np.abs(blocks).max(-1, keepdims=True)
    byte = np.maximum(np.where(amax > 0, np.frexp(amax)[1] - 1 + 127, 0) - down, 1)
    scale = np.exp2(byte - 127.0)
    codes = (blocks / scale).astype(np.float32).astype(dtype).astype(np.float64)
    return np.moveaxis((codes * scale).reshape(v.shape), -1, axis)


WIDE = False


def mx_kscale(k):
    if not WIDE:
        return np.ones(k)
    levels = np.array([10, -10, 5, -5, 0])
    if k % 512:
        return np.exp2(np.random.permutation(np.resize(levels, k // 32))).repeat(32)
    a = np.empty((k // 512, 16))
    for p in range(k // 512):
        a[p, :8] = np.random.permutation(np.resize(levels, 8))
        for g in range(8):
            far = levels[np.abs(levels - a[p, g]) >= 10]
            a[p, g + 8] = far[np.random.randint(len(far))]
    return np.exp2(a.ravel()).repeat(32)


def f64(x):
    return np.asarray(x).astype(np.float64)


def striped(idx):
    return np.tile(idx.reshape(-1, 16).T, (8, 1)).astype(np.uint16)


def unstriped(offs):
    return offs[:16].T.reshape(-1).astype(np.int64)


E2M1 = np.array([0.0, 0.5, 1.0, 1.5, 2.0, 3.0, 4.0, 6.0, -0.0, -0.5, -1.0, -1.5, -2.0, -3.0, -4.0, -6.0])


def pack_weight(w, fmt):
    k, n = w.shape
    w = f64(np.asarray(w, np.float32).astype(ml_dtypes.bfloat16)).reshape(k // 32, 32, n)
    amax = np.abs(w).max(1)
    if fmt == "e4m3":
        byte = np.frexp(amax)[1] - 1 + 127 - 7
    else:
        mant, ex = np.frexp(amax / 6.0)
        byte = np.where(mant > 0.5, ex, ex - 1) + 127
    byte = np.clip(np.where(amax > 0, byte, 1), 1, 254)
    scaled = (w * np.exp2(127.0 - byte)[:, None, :]).reshape(k, n).astype(np.float32)
    by_word = np.ascontiguousarray(scaled.reshape(k // 512, 128, 4, n).transpose(0, 1, 3, 2))
    if fmt == "e4m3":
        words = by_word.astype(ml_dtypes.float8_e4m3fn).view(np.uint8)
    else:
        c = by_word.astype(ml_dtypes.float4_e2m1fn).view(np.uint8) & 0xF
        words = (c[..., 0::2] | (c[..., 1::2] << 4)).reshape(k // 512, 128, 2 * n)
    return np.ascontiguousarray(words), np.ascontiguousarray(byte.astype(np.uint8).reshape(k // 512, 16, n))


def unpack_weight(words, scales, fmt):
    g, _, n = scales.shape
    words = np.ascontiguousarray(words).reshape(g, 128, n, -1)
    if fmt == "e4m3":
        vals = words.view(ml_dtypes.float8_e4m3fn).astype(np.float64)
    else:
        nib = np.empty((g, 128, n, 4), np.uint8)
        nib[..., 0::2] = words & 0xF
        nib[..., 1::2] = words >> 4
        vals = E2M1[nib]
    vals = vals * np.repeat(np.exp2(scales.astype(np.float64) - 127.0), 8, axis=1)[..., None]
    return vals.transpose(0, 1, 3, 2).reshape(g * 512, n)


def gelu(v):
    return 0.5 * v * (1.0 + np.tanh(np.sqrt(2.0 / np.pi) * (v + 0.044715 * v**3)))


def bf(x):
    return np.asarray(x, np.float32).astype(ml_dtypes.bfloat16)


def planes(Y):
    n, m = Y.shape
    b = f64(bf(Y)).reshape(n // 32, 32, m)
    amax = np.abs(b).max(1)
    byte = np.clip(np.where(amax > 0, np.frexp(amax)[1] - 1 + 127 - 7, 1), 1, 254)
    codes = (b * np.exp2(127.0 - byte)[:, None, :]).reshape(n, m).astype(np.float32).astype(ml_dtypes.float8_e4m3fn).view(np.uint8)
    words = codes.reshape(n // 512, 128, 4, m).transpose(0, 1, 3, 2)
    return np.ascontiguousarray(words), np.ascontiguousarray(byte.astype(np.uint8).reshape(n // 512, 16, m))


K, H, N, T, S, P = 1024, 1024, 1024, 2048, 1024, 512


def setup_inputs():
    n = np.random.standard_normal
    s = mx_kscale(K)[:, None]
    u = mx_kscale(H)[:, None]
    tab_words, tab_scales = pack_weight(n((K, T)) * s, "e4m3")
    w1 = 0.75 * n((K, H)) / np.sqrt(K) / s
    w4 = 0.25 * n((H, N)) / np.sqrt(H) * np.exp(0.8 * n(N))[None, :] / u
    w4_words, w4_scales = pack_weight(w4, "e2m1")
    opp = np.random.choice([-1.0, 1.0], H) * np.random.uniform(0.8, 2.4, H)
    return {
        "tab_words": tab_words,
        "tab_scales": tab_scales,
        "offs": striped(np.random.permutation(T)[:S]),
        "pos1": striped(np.random.permutation(S)[:P]),
        "pos2": striped(np.random.permutation(S)[:P]),
        "w1": w1.astype(np.float32),
        "sc": np.random.uniform(0.4, 1.6, H).astype(np.float32),
        "sb": (0.5 * n(H)).astype(np.float32),
        "opp": opp.astype(np.float32),
        "gain": (np.random.uniform(0.5, 1.5, H) * u[:, 0]).astype(np.float32),
        "resid": (1.2 * n((H, P)) * u).astype(np.float32),
        "w4_words": w4_words,
        "w4_scales": w4_scales,
    }


def reference(tab_words, tab_scales, offs, pos1, pos2, w1, sc, sb, opp, gain, resid, w4_words, w4_scales):
    v = unpack_weight(tab_words, tab_scales, "e4m3")[:, unstriped(offs)]
    h = mxq(f64(w1), 0, "e4m3").T @ v
    a = np.exp(f64(sc)[:, None] * h[:, unstriped(pos1)] + f64(sb)[:, None])
    c = f64(opp)[:, None] * h[:, unstriped(pos2)]
    f = f64(gain)[:, None] * (a + c) + f64(resid)
    w4 = unpack_weight(w4_words, w4_scales, "e2m1")
    y = w4.T @ mxq(f, 0, "e4m3")
    words, scales = planes(y)
    return y, words, scales

@@ -1,0 +1,350 @@
+from contextlib import ExitStack
+
+import concourse.mybir as mybir
+
+K, H, N, T, S, M = 1024, 1024, 1024, 2048, 1024, 512
+FLOPS = 2 * K * H * S + 2 * H * N * M
+
+F32 = mybir.dt.float32
+BF16 = mybir.dt.bfloat16
+I32 = mybir.dt.int32
+U32 = mybir.dt.uint32
+U16 = mybir.dt.uint16
+U8 = mybir.dt.uint8
+FP8X4 = mybir.dt.float8_e4m3fn_x4
+FP4X4 = mybir.dt.float4_e2m1fn_x4
+MULT = mybir.AluOpType.mult
+ADD = mybir.AluOpType.add
+EXP = mybir.ActivationFunctionType.Exp
+
+P = 128
+PACK = 4
+KP = P * PACK
+BANK = 512
+HALF = M // 2
+
+
+def tile_list_limb_fluid_features_kernel(
+    tc, tab_words, tab_scales, offs, pos1, pos2, w1, sc, sb, opp, gain, resid, w4_words, w4_scales, out_0, out_1, out_2
+):
+    nc = tc.nc
+    with ExitStack() as ctx:
+        keep = ctx.enter_context(tc.tile_pool(name="keep", bufs=1))
+        ring = ctx.enter_context(tc.tile_pool(name="ring", bufs=4))
+        psum = ctx.enter_context(tc.psum_pool(name="psum", bufs=1))
+
+        def sbuf(name, shape, dtype):
+            return keep.tile(shape, dtype, name=name, align_bytes=64)
+
+        def bank(k, name):
+            return psum.tile([P, BANK], F32, name=name, tag="bank%d" % k)
+
+        offs_sb = keep.tile([P, S // 16], U16, name="offs_sb")
+        pos1_sb = keep.tile([P, M // 16], U16, name="pos1_sb")
+        pos2_sb = keep.tile([P, M // 16], U16, name="pos2_sb")
+
+        tab_sc = sbuf("tab_sc", [P, T], U8)
+        nc.vector.memset(tab_sc[:].bitcast(I32), 0)
+        w4_sc_raw = sbuf("w4_sc_raw", [P, N], U8)
+        nc.gpsimd.memset(w4_sc_raw[:].bitcast(I32), 0)
+
+        tab_w = [sbuf("tab_w%d" % a, [P, T], U32) for a in range(2)]
+        w1_raw = {(b, a): sbuf("w1_raw%d%d" % (b, a), [P, PACK, KP], F32) for b in range(2) for a in range(2)}
+        resid_sb = [sbuf("resid%d" % u, [P, 2, M], F32) for u in range(4)]
+        w4_raw = sbuf("w4_raw", [P, 2, 2 * N], U8)
+
+        def load_tab(a):
+            nc.sync.dma_start(tab_w[a][:].bitcast(I32), tab_words[a].rearrange("p t i -> p (t i)").bitcast(I32))
+
+        def load_w1(b, a, j0, j1):
+            rows = w1[a * KP : (a + 1) * KP, b * KP : (b + 1) * KP].rearrange("(p j) c -> p j c", j=PACK)
+            nc.sync.dma_start(w1_raw[b, a][:, j0:j1, :], rows[:, j0:j1, :])
+
+        def load_resid(u):
+            b, t0 = u // 2, 2 * (u % 2)
+            rows = resid[b * KP : (b + 1) * KP, :].rearrange("(p t) m -> p t m", t=PACK)
+            nc.sync.dma_start(resid_sb[u][:], rows[:, t0 : t0 + 2, :])
+
+        def load_rows(name, vec):
+            tile = sbuf(name, [P, 16], F32)
+            nc.sync.dma_start(
+                tile[:].rearrange("p (b u) -> p b u", b=2)[:, :, 0:PACK], vec.rearrange("(b p t) -> p b t", b=2, t=PACK)
+            )
+            return tile
+
+        def load_planes(tile, scales):
+            for q in range(4):
+                nc.sync.dma_start(tile[32 * q : 32 * q + 8, :].bitcast(I32), scales[:, 4 * q : 4 * q + 4, :].bitcast(I32))
+
+        nc.sync.dma_start(offs_sb[:], offs)
+        load_w1(0, 0, 0, 2)
+        load_planes(tab_sc, tab_scales)
+        load_w1(0, 0, 2, 4)
+        load_tab(0)
+        load_tab(1)
+        load_w1(0, 1, 0, 4)
+        nc.sync.dma_start(pos1_sb[:], pos1)
+        nc.sync.dma_start(pos2_sb[:], pos2)
+        sc_sb = load_rows("sc_sb", sc)
+        sb_sb = load_rows("sb_sb", sb)
+        opp_sb = load_rows("opp_sb", opp)
+        gain_sb = load_rows("gain_sb", gain)
+        load_resid(0)
+        load_w1(1, 0, 0, 4)
+        load_w1(1, 1, 0, 4)
+        load_resid(1)
+        nc.sync.dma_start(w4_raw[:].bitcast(I32), w4_words.rearrange("a p c -> p a c").bitcast(I32))
+        load_planes(w4_sc_raw, w4_scales)
+        load_resid(2)
+        load_resid(3)
+
+        def col(tile, i):
+            c = 8 * (i // PACK) + i % PACK
+            return tile[:, c : c + 1]
+
+        v_sc = sbuf("v_sc", [P, S], U8)
+        v_w = [sbuf("v_w%d" % a, [P, S], U32) for a in range(2)]
+
+        def gather_words(a):
+            nc.vector.tensor_copy(v_w[a][:], tab_w[a][:].indirect(offs_sb[:]))
+
+        w1_bf = {}
+        w1_c = {}
+        w1_s = {}
+
+        def round_w1(b, a, u, copy):
+            tile = ring.tile([P, 2 * P * PACK], BF16, name="w1_bf", align_bytes=64)
+            src = w1_raw[b, a][:].rearrange("p j (m t) -> p m j t", t=PACK)[:, :, :, 2 * u : 2 * u + 2]
+            copy(tile[:].rearrange("p (t m j) -> p m j t", t=2, j=PACK), src)
+            w1_bf[b, a, u] = tile
+
+        def quant_w1(b, a, u):
+            w1_c[b, a, u] = sbuf("w1_c%d%d%d" % (b, a, u), [P, 2 * P], U32)
+            w1_s[b, a, u] = sbuf("w1_s%d%d%d" % (b, a, u), [P, 2 * P], U8)
+            nc.vector.quantize_mx(out=w1_c[b, a, u][:].bitcast(FP8X4), scales=w1_s[b, a, u][:], in_=w1_bf[b, a, u][:])
+
+        h_ps = {}
+
+        def h_pass(i, a):
+            b, t = divmod(i, PACK)
+            cols = slice((t % 2) * P, (t % 2 + 1) * P)
+            for c in range(2):
+                if a == 0:
+                    h_ps[i, c] = bank(2 * t + c, "h_ps%d%d" % (i, c))
+                sl = slice(c * BANK, (c + 1) * BANK)
+                nc.tensor.matmul_mx(
+                    out=h_ps[i, c][:],
+                    lhsT=w1_c[b, a, t // 2][:, cols].bitcast(FP8X4),
+                    lhsT_scale=w1_s[b, a, t // 2][:, cols],
+                    rhs=v_w[a][:, sl].bitcast(FP8X4),
+                    rhs_scale=v_sc[4 * a : P, sl],
+                    start=(a == 0),
+                    stop=(a == 1),
+                )
+
+        h_sb = [sbuf("h%d" % i, [P, S], F32) for i in range(8)]
+        g_sb = [sbuf("g%d" % i, [P, M], F32) for i in range(8)]
+        a_sb = {}
+        u_sb = {}
+        spans = {"all": (0, M), 0: (0, HALF), 1: (HALF, HALF)}
+        f_pl = {(b, hf): sbuf("f_pl%d%s" % (b, hf), [P, PACK * spans[hf][1]], BF16) for b, hf in ((0, "all"), (1, 0), (1, 1))}
+
+        def h_out(i, c, copy):
+            copy(h_sb[i][:, c * BANK : (c + 1) * BANK], h_ps[i, c][:])
+
+        def look(i, hf):
+            m0, w = spans[hf]
+            a_sb[i, hf] = sbuf("a%d%s" % (i, hf), [P, w], F32)
+            nc.scalar.activation(
+                out=a_sb[i, hf][:],
+                in_=h_sb[i][:].indirect(pos1_sb[:, m0 // 16 : (m0 + w) // 16]),
+                func=EXP,
+                bias=col(sb_sb, i),
+                scale=col(sc_sb, i),
+            )
+
+        def pick(i):
+            nc.vector.tensor_copy(g_sb[i][:], h_sb[i][:].indirect(pos2_sb[:]))
+
+        def join(i, hf):
+            m0, w = spans[hf]
+            u_sb[i, hf] = ring.tile([P, w], F32, name="u", align_bytes=64)
+            nc.vector.scalar_tensor_tensor(
+                u_sb[i, hf][:], g_sb[i][:, m0 : m0 + w], col(opp_sb, i), a_sb[i, hf][:], MULT, ADD
+            )
+
+        def finish(i, hf):
+            m0, w = spans[hf]
+            b, t = divmod(i, PACK)
+            nc.vector.scalar_tensor_tensor(
+                f_pl[b, hf][:, t * w : (t + 1) * w],
+                u_sb[i, hf][:],
+                col(gain_sb, i),
+                resid_sb[i // 2][:, i % 2, m0 : m0 + w],
+                MULT,
+                ADD,
+            )
+
+        def weave(name, planar, w, copy):
+            tile = sbuf(name, [P, PACK * w], BF16)
+            copy(
+                tile[:].rearrange("p (c i t) -> p c t i", i=4, t=PACK),
+                planar[:].rearrange("p (t c i) -> p c t i", i=4, t=PACK),
+            )
+            return tile
+
+        f_wv = {}
+        f_c = [sbuf("f_c%d" % b, [P, M], U32) for b in range(2)]
+        f_s = [sbuf("f_s%d" % b, [P, M], U8) for b in range(2)]
+
+        def weave_f(b, hf, copy):
+            f_wv[b, hf] = weave("f_wv%d%s" % (b, hf), f_pl[b, hf], spans[hf][1], copy)
+
+        def quant_f(b, hf):
+            m0, w = spans[hf]
+            nc.vector.quantize_mx(
+                out=f_c[b][:, m0 : m0 + w].bitcast(FP8X4), scales=f_s[b][:, m0 : m0 + w], in_=f_wv[b, hf][:]
+            )
+
+        w4_w = [sbuf("w4_w%d" % a, [P, 2 * N], U8) for a in range(2)]
+        w4_s = [sbuf("w4_s%d" % a, [P, N], U8) for a in range(2)]
+
+        def deal_w4_words(a):
+            nc.scalar.copy(
+                w4_w[a][:].bitcast(U16).rearrange("p (g t m) -> p g t m", t=PACK, m=P),
+                w4_raw[:, a, :].bitcast(U16).rearrange("p (g m t) -> p g t m", t=PACK, m=P),
+            )
+
+        def deal_w4_scales():
+            nc.vector.tensor_copy(
+                w4_s[0][:].rearrange("p (g t m) -> p g t m", t=PACK, m=P),
+                w4_sc_raw[:].rearrange("p (g m t) -> p g t m", t=PACK, m=P),
+            )
+            for q in range(4):
+                nc.sync.dma_start(
+                    w4_s[1][32 * q : 32 * q + 4, :].bitcast(I32), w4_s[0][32 * q + 4 : 32 * q + 8, :].bitcast(I32)
+                )
+
+        y_ps = {}
+
+        def y_pass(hf, a):
+            for g in range(2):
+                for t in range(PACK):
+                    k = 2 * g + t // 2
+                    if a == 0 and t % 2 == 0:
+                        y_ps[hf, k] = bank(4 * hf + k, "y_ps%d%d" % (hf, k))
+                    n0 = (g * PACK + t) * P
+                    nc.tensor.matmul_mx(
+                        out=y_ps[hf, k][:, (t % 2) * HALF : (t % 2 + 1) * HALF],
+                        lhsT=w4_w[a][:, 2 * n0 : 2 * (n0 + P)].bitcast(FP4X4),
+                        lhsT_scale=w4_s[a][:, n0 : n0 + P],
+                        rhs=f_c[a][:, hf * HALF : (hf + 1) * HALF].bitcast(FP8X4),
+                        rhs_scale=f_s[a][:, hf * HALF : (hf + 1) * HALF],
+                        start=(a == 0 and t % 2 == 0),
+                        stop=(a == 1 and t % 2 == 1),
+                    )
+
+        y_sb = {(hf, g): sbuf("y%d%d" % (hf, g), [P, PACK * HALF], F32) for hf in range(2) for g in range(2)}
+        y_c = {(hf, g): sbuf("y_c%d%d" % (hf, g), [P, HALF], U32) for hf in range(2) for g in range(2)}
+        y_s = sbuf("y_s", [P, 2 * M], U8)
+        y_wv = {}
+
+        def y_out(hf, k, copy):
+            g, u = divmod(k, 2)
+            part = y_sb[hf, g][:, u * BANK : (u + 1) * BANK]
+            copy(part, y_ps[hf, k][:])
+            rows = out_0[g * KP : (g + 1) * KP, hf * HALF : (hf + 1) * HALF].rearrange("(p t) m -> p t m", t=PACK)
+            nc.sync.dma_start(rows[:, 2 * u : 2 * u + 2, :], part.rearrange("p (t m) -> p t m", t=2))
+
+        def weave_y(hf, g, copy):
+            y_wv[hf, g] = weave("y_wv%d%d" % (hf, g), y_sb[hf, g], HALF, copy)
+
+        def quant_y(hf, g):
+            c0 = g * M + hf * HALF
+            nc.vector.quantize_mx(out=y_c[hf, g][:].bitcast(FP8X4), scales=y_s[:, c0 : c0 + HALF], in_=y_wv[hf, g][:])
+            words = out_1[g].rearrange("p m t -> p (m t)").bitcast(I32)
+            nc.sync.dma_start(words[:, hf * HALF : (hf + 1) * HALF], y_c[hf, g][:].bitcast(I32))
+
+        on_s = nc.scalar.copy
+        on_v = nc.vector.tensor_copy
+
+        nc.vector.tensor_copy(v_sc[:], tab_sc[:].indirect(offs_sb[:]))
+        round_w1(0, 0, 0, on_s)
+        round_w1(0, 0, 1, on_v)
+        quant_w1(0, 0, 0)
+        quant_w1(0, 0, 1)
+        gather_words(0)
+        for t in range(PACK):
+            h_pass(t, 0)
+        gather_words(1)
+        round_w1(0, 1, 0, on_v)
+        round_w1(0, 1, 1, on_s)
+        quant_w1(0, 1, 0)
+        h_pass(0, 1)
+        h_pass(1, 1)
+        quant_w1(0, 1, 1)
+        h_pass(2, 1)
+        h_pass(3, 1)
+
+        for i in range(8):
+            hf = "all" if i < PACK else 0
+            h_out(i, 0, on_s)
+            h_out(i, 1, on_v if i == 0 else on_s)
+            look(i, hf)
+            pick(i)
+            if i > 0:
+                finish(i - 1, "all" if i - 1 < PACK else 0)
+            if i < 2:
+                round_w1(1, i, 0, on_v)
+                round_w1(1, i, 1, on_s)
+            join(i, hf)
+            if i < 2:
+                quant_w1(1, i, 0)
+                quant_w1(1, i, 1)
+            if 1 <= i < 5:
+                h_pass(i + 3, 0)
+                h_pass(i + 3, 1)
+            if i == 4:
+                weave_f(0, "all", on_v)
+                deal_w4_words(0)
+            if i == 5:
+                quant_f(0, "all")
+                deal_w4_scales()
+            if i == 6:
+                deal_w4_words(1)
+        y_pass(0, 0)
+        y_pass(1, 0)
+
+        for i in range(4, 8):
+            look(i, 1)
+            if i == 4:
+                finish(7, 0)
+                weave_f(1, 0, on_v)
+                join(i, 1)
+                quant_f(1, 0)
+                y_pass(0, 1)
+            else:
+                finish(i - 1, 1)
+                join(i, 1)
+        for k in range(4):
+            y_out(0, k, on_s)
+        weave_y(0, 0, on_s)
+        finish(7, 1)
+        weave_f(1, 1, on_v)
+        weave_y(0, 1, on_v)
+        quant_f(1, 1)
+        y_pass(1, 1)
+        quant_y(0, 1)
+        quant_y(0, 0)
+        for k in range(4):
+            y_out(1, k, on_s)
+        weave_y(1, 0, on_v)
+        quant_y(1, 0)
+        weave_y(1, 1, on_v)
+        quant_y(1, 1)
+        for q in range(4):
+            queue = nc.scalar if q % 2 else nc.sync
+            queue.dma_start(
+                out_2[:, 4 * q : 4 * q + 4, :].rearrange("g r m -> r g m").bitcast(I32),
+                y_s[32 * q : 32 * q + 4, :].rearrange("r (g m) -> r g m", g=2).bitcast(I32),
+            )

@@ -53,8 +53,9 @@ def tile_list_limb_fluid_features_kernel(
         resid_sb = [sbuf("resid%d" % u, [P, 2, M], F32) for u in range(4)]
         w4_raw = sbuf("w4_raw", [P, 2, 2 * N], U8)
 
-        def load_tab(a):
-            nc.sync.dma_start(tab_w[a][:].bitcast(I32), tab_words[a].rearrange("p t i -> p (t i)").bitcast(I32))
+        def load_tab(a, c0, c1):
+            words = tab_words[a].rearrange("p t i -> p (t i)").bitcast(I32)
+            nc.sync.dma_start(tab_w[a][:, c0:c1].bitcast(I32), words[:, c0:c1])
 
         def load_w1(b, a, j0, j1):
             rows = w1[a * KP : (a + 1) * KP, b * KP : (b + 1) * KP].rearrange("(p j) c -> p j c", j=PACK)
@@ -77,11 +78,11 @@ def tile_list_limb_fluid_features_kernel(
                 nc.sync.dma_start(tile[32 * q : 32 * q + 8, :].bitcast(I32), scales[:, 4 * q : 4 * q + 4, :].bitcast(I32))
 
         nc.sync.dma_start(offs_sb[:], offs)
-        load_w1(0, 0, 0, 2)
+        load_tab(0, 0, T // 2)
         load_planes(tab_sc, tab_scales)
-        load_w1(0, 0, 2, 4)
-        load_tab(0)
-        load_tab(1)
+        load_tab(0, T // 2, T)
+        load_tab(1, 0, T)
+        load_w1(0, 0, 0, 4)
         load_w1(0, 1, 0, 4)
         nc.sync.dma_start(pos1_sb[:], pos1)
         nc.sync.dma_start(pos2_sb[:], pos2)
@@ -130,7 +131,7 @@ def tile_list_limb_fluid_features_kernel(
             cols = slice((t % 2) * P, (t % 2 + 1) * P)
             for c in range(2):
                 if a == 0:
-                    h_ps[i, c] = bank(2 * t + c, "h_ps%d%d" % (i, c))
+                    h_ps[i, c] = bank(2 * (i % 2) + c, "h_ps%d%d" % (i, c))
                 sl = slice(c * BANK, (c + 1) * BANK)
                 nc.tensor.matmul_mx(
                     out=h_ps[i, c][:],
@@ -154,7 +155,7 @@ def tile_list_limb_fluid_features_kernel(
 
         def look(i, hf):
             m0, w = spans[hf]
-            a_sb[i, hf] = sbuf("a%d%s" % (i, hf), [P, w], F32)
+            a_sb[i, hf] = keep.tile([P, w], F32, name="a%d%s" % (i, hf), align_bytes=64)
             nc.scalar.activation(
                 out=a_sb[i, hf][:],
                 in_=h_sb[i][:].indirect(pos1_sb[:, m0 // 16 : (m0 + w) // 16]),
@@ -185,11 +186,12 @@ def tile_list_limb_fluid_features_kernel(
                 ADD,
             )
 
-        def weave(name, planar, w, copy):
-            tile = sbuf(name, [P, PACK * w], BF16)
+        def weave(name, planar, copy, tag=None):
+            w = planar.shape[2]
+            tile = keep.tile([P, PACK * w], BF16, name=name, tag=tag or name, align_bytes=64)
             copy(
                 tile[:].rearrange("p (c i t) -> p c t i", i=4, t=PACK),
-                planar[:].rearrange("p (t c i) -> p c t i", i=4, t=PACK),
+                planar.rearrange("p t (c i) -> p c t i", i=4),
             )
             return tile
 
@@ -197,13 +199,15 @@ def tile_list_limb_fluid_features_kernel(
         f_c = [sbuf("f_c%d" % b, [P, M], U32) for b in range(2)]
         f_s = [sbuf("f_s%d" % b, [P, M], U8) for b in range(2)]
 
-        def weave_f(b, hf, copy):
-            f_wv[b, hf] = weave("f_wv%d%s" % (b, hf), f_pl[b, hf], spans[hf][1], copy)
+        def weave_f(b, m0, w, copy, tag=None):
+            hf = "all" if b == 0 else m0 // HALF
+            c0 = m0 - spans[hf][0]
+            planar = f_pl[b, hf][:].rearrange("p (t m) -> p t m", t=PACK)[:, :, c0 : c0 + w]
+            f_wv[b, m0] = weave("f_wv%d_%d" % (b, m0), planar, copy, tag)
 
-        def quant_f(b, hf):
-            m0, w = spans[hf]
+        def quant_f(b, m0, w):
             nc.vector.quantize_mx(
-                out=f_c[b][:, m0 : m0 + w].bitcast(FP8X4), scales=f_s[b][:, m0 : m0 + w], in_=f_wv[b, hf][:]
+                out=f_c[b][:, m0 : m0 + w].bitcast(FP8X4), scales=f_s[b][:, m0 : m0 + w], in_=f_wv[b, m0][:]
             )
 
         w4_w = [sbuf("w4_w%d" % a, [P, 2 * N], U8) for a in range(2)]
@@ -226,122 +230,132 @@ def tile_list_limb_fluid_features_kernel(
                 )
 
         y_ps = {}
+        pieces = ((0, 256), (256, 256))
+        first_bank = {}
+        nb = 4
+        for m0, w in pieces:
+            first_bank[m0] = nb
+            nb = (nb + 2 * PACK * w // BANK) % 8
 
-        def y_pass(hf, a):
-            for g in range(2):
-                for t in range(PACK):
-                    k = 2 * g + t // 2
-                    if a == 0 and t % 2 == 0:
-                        y_ps[hf, k] = bank(4 * hf + k, "y_ps%d%d" % (hf, k))
-                    n0 = (g * PACK + t) * P
-                    nc.tensor.matmul_mx(
-                        out=y_ps[hf, k][:, (t % 2) * HALF : (t % 2 + 1) * HALF],
-                        lhsT=w4_w[a][:, 2 * n0 : 2 * (n0 + P)].bitcast(FP4X4),
-                        lhsT_scale=w4_s[a][:, n0 : n0 + P],
-                        rhs=f_c[a][:, hf * HALF : (hf + 1) * HALF].bitcast(FP8X4),
-                        rhs_scale=f_s[a][:, hf * HALF : (hf + 1) * HALF],
-                        start=(a == 0 and t % 2 == 0),
-                        stop=(a == 1 and t % 2 == 1),
-                    )
+        def y_pass(m0, w, a):
+            per_bank = BANK // w
+            for n in range(2 * PACK):
+                k, u = divmod(n, per_bank)
+                if a == 0 and u == 0:
+                    y_ps[m0, k] = bank(first_bank[m0] + k, "y_ps%d_%d" % (m0, k))
+                n0 = n * P
+                nc.tensor.matmul_mx(
+                    out=y_ps[m0, k][:, u * w : (u + 1) * w],
+                    lhsT=w4_w[a][:, 2 * n0 : 2 * (n0 + P)].bitcast(FP4X4),
+                    lhsT_scale=w4_s[a][:, n0 : n0 + P],
+                    rhs=f_c[a][:, m0 : m0 + w].bitcast(FP8X4),
+                    rhs_scale=f_s[a][:, m0 : m0 + w],
+                    start=(a == 0 and u == 0),
+                    stop=(a == 1 and u == per_bank - 1),
+                )
 
-        y_sb = {(hf, g): sbuf("y%d%d" % (hf, g), [P, PACK * HALF], F32) for hf in range(2) for g in range(2)}
-        y_c = {(hf, g): sbuf("y_c%d%d" % (hf, g), [P, HALF], U32) for hf in range(2) for g in range(2)}
+        y_sb = {(m0, g): sbuf("y%d_%d" % (m0, g), [P, PACK * w], F32) for m0, w in pieces for g in range(2)}
+        y_c = {(m0, g): sbuf("y_c%d_%d" % (m0, g), [P, w], U32) for m0, w in pieces for g in range(2)}
         y_s = sbuf("y_s", [P, 2 * M], U8)
         y_wv = {}
 
-        def y_out(hf, k, copy):
-            g, u = divmod(k, 2)
-            part = y_sb[hf, g][:, u * BANK : (u + 1) * BANK]
-            copy(part, y_ps[hf, k][:])
-            rows = out_0[g * KP : (g + 1) * KP, hf * HALF : (hf + 1) * HALF].rearrange("(p t) m -> p t m", t=PACK)
-            nc.sync.dma_start(rows[:, 2 * u : 2 * u + 2, :], part.rearrange("p (t m) -> p t m", t=2))
+        def y_out(m0, w, k, copy):
+            per_bank = BANK // w
+            g, t0 = divmod(k * per_bank, PACK)
+            part = y_sb[m0, g][:, t0 * w : (t0 + per_bank) * w]
+            copy(part, y_ps[m0, k][:])
+            rows = out_0[g * KP : (g + 1) * KP, m0 : m0 + w].rearrange("(p t) m -> p t m", t=PACK)
+            nc.sync.dma_start(rows[:, t0 : t0 + per_bank, :], part.rearrange("p (t m) -> p t m", m=w))
 
-        def weave_y(hf, g, copy):
-            y_wv[hf, g] = weave("y_wv%d%d" % (hf, g), y_sb[hf, g], HALF, copy)
+        def weave_y(m0, g, copy):
+            planar = y_sb[m0, g][:].rearrange("p (t m) -> p t m", t=PACK)
+            y_wv[m0, g] = weave("y_wv%d_%d" % (m0, g), planar, copy)
 
-        def quant_y(hf, g):
-            c0 = g * M + hf * HALF
-            nc.vector.quantize_mx(out=y_c[hf, g][:].bitcast(FP8X4), scales=y_s[:, c0 : c0 + HALF], in_=y_wv[hf, g][:])
+        def quant_y(m0, w, g):
+            c0 = g * M + m0
+            nc.vector.quantize_mx(out=y_c[m0, g][:].bitcast(FP8X4), scales=y_s[:, c0 : c0 + w], in_=y_wv[m0, g][:])
             words = out_1[g].rearrange("p m t -> p (m t)").bitcast(I32)
-            nc.sync.dma_start(words[:, hf * HALF : (hf + 1) * HALF], y_c[hf, g][:].bitcast(I32))
+            nc.sync.dma_start(words[:, m0 : m0 + w], y_c[m0, g][:].bitcast(I32))
 
         on_s = nc.scalar.copy
         on_v = nc.vector.tensor_copy
 
         nc.vector.tensor_copy(v_sc[:], tab_sc[:].indirect(offs_sb[:]))
-        round_w1(0, 0, 0, on_s)
-        round_w1(0, 0, 1, on_v)
-        quant_w1(0, 0, 0)
-        quant_w1(0, 0, 1)
         gather_words(0)
-        for t in range(PACK):
-            h_pass(t, 0)
         gather_words(1)
+        round_w1(0, 0, 0, on_s)
+        round_w1(0, 0, 1, on_s)
+        quant_w1(0, 0, 0)
+        h_pass(0, 0)
+        h_pass(1, 0)
         round_w1(0, 1, 0, on_v)
         round_w1(0, 1, 1, on_s)
+        quant_w1(0, 0, 1)
         quant_w1(0, 1, 0)
         h_pass(0, 1)
         h_pass(1, 1)
         quant_w1(0, 1, 1)
-        h_pass(2, 1)
-        h_pass(3, 1)
 
+        casts = [(0, on_v), (0, on_v), (1, on_v), (1, on_s)]
         for i in range(8):
-            hf = "all" if i < PACK else 0
             h_out(i, 0, on_s)
             h_out(i, 1, on_v if i == 0 else on_s)
-            look(i, hf)
+            look(i, "all" if i < PACK else 0)
             pick(i)
             if i > 0:
                 finish(i - 1, "all" if i - 1 < PACK else 0)
-            if i < 2:
-                round_w1(1, i, 0, on_v)
-                round_w1(1, i, 1, on_s)
-            join(i, hf)
-            if i < 2:
-                quant_w1(1, i, 0)
-                quant_w1(1, i, 1)
-            if 1 <= i < 5:
-                h_pass(i + 3, 0)
-                h_pass(i + 3, 1)
+            for n, (at, eng) in enumerate(casts):
+                if at == i:
+                    round_w1(1, n // 2, n % 2, eng)
+            join(i, "all" if i < PACK else 0)
+            for n, (at, eng) in enumerate(casts):
+                if at == i:
+                    quant_w1(1, n // 2, n % 2)
+            if i < 6:
+                h_pass(i + 2, 0)
+                h_pass(i + 2, 1)
+            if i == 5:
+                deal_w4_scales()
             if i == 4:
-                weave_f(0, "all", on_v)
                 deal_w4_words(0)
             if i == 5:
-                quant_f(0, "all")
-                deal_w4_scales()
-            if i == 6:
                 deal_w4_words(1)
-        y_pass(0, 0)
-        y_pass(1, 0)
-
+        weave_f(0, 0, HALF, on_s, None)
+        finish(7, 0)
+        quant_f(0, 0, HALF)
+        y_pass(0, HALF, 0)
+        weave_f(1, 0, HALF, on_v)
         for i in range(4, 8):
             look(i, 1)
-            if i == 4:
-                finish(7, 0)
-                weave_f(1, 0, on_v)
-                join(i, 1)
-                quant_f(1, 0)
-                y_pass(0, 1)
-            else:
+            if i > 4:
                 finish(i - 1, 1)
-                join(i, 1)
+            join(i, 1)
+            if i == 4:
+                quant_f(1, 0, HALF)
+                y_pass(0, HALF, 1)
+        weave_f(0, HALF, HALF, on_s, "a70")
         for k in range(4):
-            y_out(0, k, on_s)
-        weave_y(0, 0, on_s)
+            y_out(0, HALF, k, on_s)
         finish(7, 1)
-        weave_f(1, 1, on_v)
+        quant_f(0, HALF, HALF)
+        y_pass(HALF, HALF, 0)
+        weave_f(1, HALF, HALF, on_v)
+        weave_y(0, 0, on_v)
+        quant_f(1, HALF, HALF)
+        y_pass(HALF, HALF, 1)
         weave_y(0, 1, on_v)
-        quant_f(1, 1)
-        y_pass(1, 1)
-        quant_y(0, 1)
-        quant_y(0, 0)
-        for k in range(4):
-            y_out(1, k, on_s)
-        weave_y(1, 0, on_v)
-        quant_y(1, 0)
-        weave_y(1, 1, on_v)
-        quant_y(1, 1)
+        quant_y(0, HALF, 0)
+        quant_y(0, HALF, 1)
+        n = 0
+        for m0, w in pieces[1:]:
+            for k in range(2 * PACK * w // BANK):
+                y_out(m0, w, k, on_v if n in () else on_s)
+                n = n + 1
+        for m0, w in pieces[1:]:
+            for g in range(2):
+                weave_y(m0, g, on_v)
+            for g in range(2):
+                quant_y(m0, w, g)
         for q in range(4):
             queue = nc.scalar if q % 2 else nc.sync
             queue.dma_start(

@@ -16,12 +16,14 @@ FP4X4 = mybir.dt.float4_e2m1fn_x4
 MULT = mybir.AluOpType.mult
 ADD = mybir.AluOpType.add
 EXP = mybir.ActivationFunctionType.Exp
+COPY = mybir.ActivationFunctionType.Copy
 
 P = 128
 PACK = 4
 KP = P * PACK
 BANK = 512
 HALF = M // 2
+TILES = H // P
 
 
 def tile_list_limb_fluid_features_kernel(
@@ -30,7 +32,6 @@ def tile_list_limb_fluid_features_kernel(
     nc = tc.nc
     with ExitStack() as ctx:
         keep = ctx.enter_context(tc.tile_pool(name="keep", bufs=1))
-        ring = ctx.enter_context(tc.tile_pool(name="ring", bufs=4))
         psum = ctx.enter_context(tc.psum_pool(name="psum", bufs=1))
 
         def sbuf(name, shape, dtype):
@@ -38,6 +39,9 @@ def tile_list_limb_fluid_features_kernel(
 
         def bank(k, name):
             return psum.tile([P, BANK], F32, name=name, tag="bank%d" % k)
+
+        on_s = nc.scalar.copy
+        on_v = nc.vector.tensor_copy
 
         offs_sb = keep.tile([P, S // 16], U16, name="offs_sb")
         pos1_sb = keep.tile([P, M // 16], U16, name="pos1_sb")
@@ -50,25 +54,24 @@ def tile_list_limb_fluid_features_kernel(
 
         tab_w = [sbuf("tab_w%d" % a, [P, T], U32) for a in range(2)]
         w1_raw = {(b, a): sbuf("w1_raw%d%d" % (b, a), [P, PACK, KP], F32) for b in range(2) for a in range(2)}
-        resid_sb = [sbuf("resid%d" % u, [P, 2, M], F32) for u in range(4)]
+        base = [sbuf("base%d" % b, [P, PACK, M], F32) for b in range(2)]
         w4_raw = sbuf("w4_raw", [P, 2, 2 * N], U8)
 
         def load_tab(a, c0, c1):
             words = tab_words[a].rearrange("p t i -> p (t i)").bitcast(I32)
             nc.sync.dma_start(tab_w[a][:, c0:c1].bitcast(I32), words[:, c0:c1])
 
-        def load_w1(b, a, j0, j1):
-            rows = w1[a * KP : (a + 1) * KP, b * KP : (b + 1) * KP].rearrange("(p j) c -> p j c", j=PACK)
-            nc.sync.dma_start(w1_raw[b, a][:, j0:j1, :], rows[:, j0:j1, :])
+        def load_w1(b, a):
+            rows = w1[a * KP : (a + 1) * KP, b * KP : (b + 1) * KP]
+            nc.sync.dma_start(w1_raw[b, a][:], rows.rearrange("(p j) c -> p j c", j=PACK))
 
-        def load_resid(u):
-            b, t0 = u // 2, 2 * (u % 2)
+        def load_resid(b, t0, t1):
             rows = resid[b * KP : (b + 1) * KP, :].rearrange("(p t) m -> p t m", t=PACK)
-            nc.sync.dma_start(resid_sb[u][:], rows[:, t0 : t0 + 2, :])
+            nc.sync.dma_start(base[b][:, t0:t1, :], rows[:, t0:t1, :])
 
-        def load_rows(name, vec):
+        def load_rows(name, vec, queue):
             tile = sbuf(name, [P, 16], F32)
-            nc.sync.dma_start(
+            queue.dma_start(
                 tile[:].rearrange("p (b u) -> p b u", b=2)[:, :, 0:PACK], vec.rearrange("(b p t) -> p b t", b=2, t=PACK)
             )
             return tile
@@ -77,44 +80,45 @@ def tile_list_limb_fluid_features_kernel(
             for q in range(4):
                 nc.sync.dma_start(tile[32 * q : 32 * q + 8, :].bitcast(I32), scales[:, 4 * q : 4 * q + 4, :].bitcast(I32))
 
+        opp_sb = load_rows("opp_sb", opp, nc.sync)
+        gain_sb = load_rows("gain_sb", gain, nc.sync)
         nc.sync.dma_start(offs_sb[:], offs)
         load_tab(0, 0, T // 2)
         load_planes(tab_sc, tab_scales)
         load_tab(0, T // 2, T)
         load_tab(1, 0, T)
-        load_w1(0, 0, 0, 4)
-        load_w1(0, 1, 0, 4)
+        load_w1(0, 0)
+        load_w1(0, 1)
         nc.sync.dma_start(pos1_sb[:], pos1)
         nc.sync.dma_start(pos2_sb[:], pos2)
-        sc_sb = load_rows("sc_sb", sc)
-        sb_sb = load_rows("sb_sb", sb)
-        opp_sb = load_rows("opp_sb", opp)
-        gain_sb = load_rows("gain_sb", gain)
-        load_resid(0)
-        load_w1(1, 0, 0, 4)
-        load_w1(1, 1, 0, 4)
-        load_resid(1)
+        sc_sb = load_rows("sc_sb", sc, nc.sync)
+        sb_sb = load_rows("sb_sb", sb, nc.sync)
+        load_resid(0, 0, 2)
+        load_w1(1, 0)
+        load_w1(1, 1)
+        load_resid(0, 2, 4)
         nc.sync.dma_start(w4_raw[:].bitcast(I32), w4_words.rearrange("a p c -> p a c").bitcast(I32))
         load_planes(w4_sc_raw, w4_scales)
-        load_resid(2)
-        load_resid(3)
+        load_resid(1, 0, 4)
 
         def col(tile, i):
             c = 8 * (i // PACK) + i % PACK
             return tile[:, c : c + 1]
 
+        weight = [sbuf("weight%d" % i, [P, M], F32) for i in range(TILES)]
+        for i in range(TILES):
+            nc.scalar.activation(
+                out=weight[i][:], in_=col(opp_sb, i).to_broadcast([P, M]), func=COPY, scale=col(gain_sb, i)
+            )
+
         v_sc = sbuf("v_sc", [P, S], U8)
         v_w = [sbuf("v_w%d" % a, [P, S], U32) for a in range(2)]
-
-        def gather_words(a):
-            nc.vector.tensor_copy(v_w[a][:], tab_w[a][:].indirect(offs_sb[:]))
-
         w1_bf = {}
         w1_c = {}
         w1_s = {}
 
         def round_w1(b, a, u, copy):
-            tile = ring.tile([P, 2 * P * PACK], BF16, name="w1_bf", align_bytes=64)
+            tile = keep.tile([P, 2 * P * PACK], BF16, name="w1_bf", bufs=4, align_bytes=64)
             src = w1_raw[b, a][:].rearrange("p j (m t) -> p m j t", t=PACK)[:, :, :, 2 * u : 2 * u + 2]
             copy(tile[:].rearrange("p (t m j) -> p m j t", t=2, j=PACK), src)
             w1_bf[b, a, u] = tile
@@ -143,21 +147,17 @@ def tile_list_limb_fluid_features_kernel(
                     stop=(a == 1),
                 )
 
-        h_sb = [sbuf("h%d" % i, [P, S], F32) for i in range(8)]
-        g_sb = [sbuf("g%d" % i, [P, M], F32) for i in range(8)]
-        a_sb = {}
-        u_sb = {}
-        spans = {"all": (0, M), 0: (0, HALF), 1: (HALF, HALF)}
-        f_pl = {(b, hf): sbuf("f_pl%d%s" % (b, hf), [P, PACK * spans[hf][1]], BF16) for b, hf in ((0, "all"), (1, 0), (1, 1))}
+        h_sb = [sbuf("h%d" % i, [P, S], F32) for i in range(TILES)]
+        picked = [sbuf("picked%d" % b, [P, PACK, M], F32) for b in range(2)]
+        looked = {}
 
         def h_out(i, c, copy):
             copy(h_sb[i][:, c * BANK : (c + 1) * BANK], h_ps[i, c][:])
 
-        def look(i, hf):
-            m0, w = spans[hf]
-            a_sb[i, hf] = keep.tile([P, w], F32, name="a%d%s" % (i, hf), align_bytes=64)
+        def look(i, m0, w):
+            looked[i, m0] = sbuf("looked%d_%d" % (i, m0), [P, w], F32)
             nc.scalar.activation(
-                out=a_sb[i, hf][:],
+                out=looked[i, m0][:],
                 in_=h_sb[i][:].indirect(pos1_sb[:, m0 // 16 : (m0 + w) // 16]),
                 func=EXP,
                 bias=col(sb_sb, i),
@@ -165,49 +165,33 @@ def tile_list_limb_fluid_features_kernel(
             )
 
         def pick(i):
-            nc.vector.tensor_copy(g_sb[i][:], h_sb[i][:].indirect(pos2_sb[:]))
-
-        def join(i, hf):
-            m0, w = spans[hf]
-            u_sb[i, hf] = ring.tile([P, w], F32, name="u", align_bytes=64)
-            nc.vector.scalar_tensor_tensor(
-                u_sb[i, hf][:], g_sb[i][:, m0 : m0 + w], col(opp_sb, i), a_sb[i, hf][:], MULT, ADD
-            )
-
-        def finish(i, hf):
-            m0, w = spans[hf]
             b, t = divmod(i, PACK)
-            nc.vector.scalar_tensor_tensor(
-                f_pl[b, hf][:, t * w : (t + 1) * w],
-                u_sb[i, hf][:],
-                col(gain_sb, i),
-                resid_sb[i // 2][:, i % 2, m0 : m0 + w],
-                MULT,
-                ADD,
-            )
+            nc.vector.tensor_tensor(picked[b][:, t, :], h_sb[i][:].indirect(pos2_sb[:]), weight[i][:], MULT)
 
-        def weave(name, planar, copy, tag=None):
-            w = planar.shape[2]
-            tile = keep.tile([P, PACK * w], BF16, name=name, tag=tag or name, align_bytes=64)
-            copy(
-                tile[:].rearrange("p (c i t) -> p c t i", i=4, t=PACK),
-                planar.rearrange("p t (c i) -> p c t i", i=4),
-            )
-            return tile
+        def add_look(i, m0, w):
+            b, t = divmod(i, PACK)
+            part = base[b][:, t, m0 : m0 + w]
+            nc.vector.scalar_tensor_tensor(part, looked[i, m0][:], col(gain_sb, i), part, MULT, ADD)
 
-        f_wv = {}
+        def woven(tile):
+            return tile[:].rearrange("p (c i t) -> p c t i", i=2, t=PACK)
+
+        def planar(rows):
+            return rows.rearrange("p t (c i) -> p c t i", i=2)
+
+        f_bf = {}
         f_c = [sbuf("f_c%d" % b, [P, M], U32) for b in range(2)]
         f_s = [sbuf("f_s%d" % b, [P, M], U8) for b in range(2)]
 
-        def weave_f(b, m0, w, copy, tag=None):
-            hf = "all" if b == 0 else m0 // HALF
-            c0 = m0 - spans[hf][0]
-            planar = f_pl[b, hf][:].rearrange("p (t m) -> p t m", t=PACK)[:, :, c0 : c0 + w]
-            f_wv[b, m0] = weave("f_wv%d_%d" % (b, m0), planar, copy, tag)
+        def finish_f(b, m0, w):
+            f_bf[b, m0] = sbuf("f_bf%d_%d" % (b, m0), [P, PACK * w], BF16)
+            nc.vector.tensor_tensor(
+                woven(f_bf[b, m0]), planar(picked[b][:, :, m0 : m0 + w]), planar(base[b][:, :, m0 : m0 + w]), ADD
+            )
 
         def quant_f(b, m0, w):
             nc.vector.quantize_mx(
-                out=f_c[b][:, m0 : m0 + w].bitcast(FP8X4), scales=f_s[b][:, m0 : m0 + w], in_=f_wv[b, m0][:]
+                out=f_c[b][:, m0 : m0 + w].bitcast(FP8X4), scales=f_s[b][:, m0 : m0 + w], in_=f_bf[b, m0][:]
             )
 
         w4_w = [sbuf("w4_w%d" % a, [P, 2 * N], U8) for a in range(2)]
@@ -230,59 +214,50 @@ def tile_list_limb_fluid_features_kernel(
                 )
 
         y_ps = {}
-        pieces = ((0, 256), (256, 256))
-        first_bank = {}
-        nb = 4
-        for m0, w in pieces:
-            first_bank[m0] = nb
-            nb = (nb + 2 * PACK * w // BANK) % 8
 
-        def y_pass(m0, w, a):
-            per_bank = BANK // w
+        def y_pass(hf, a):
             for n in range(2 * PACK):
-                k, u = divmod(n, per_bank)
+                k, u = divmod(n, 2)
                 if a == 0 and u == 0:
-                    y_ps[m0, k] = bank(first_bank[m0] + k, "y_ps%d_%d" % (m0, k))
-                n0 = n * P
+                    y_ps[hf, k] = bank(4 * (1 - hf) + k, "y_ps%d_%d" % (hf, k))
                 nc.tensor.matmul_mx(
-                    out=y_ps[m0, k][:, u * w : (u + 1) * w],
-                    lhsT=w4_w[a][:, 2 * n0 : 2 * (n0 + P)].bitcast(FP4X4),
-                    lhsT_scale=w4_s[a][:, n0 : n0 + P],
-                    rhs=f_c[a][:, m0 : m0 + w].bitcast(FP8X4),
-                    rhs_scale=f_s[a][:, m0 : m0 + w],
+                    out=y_ps[hf, k][:, u * HALF : (u + 1) * HALF],
+                    lhsT=w4_w[a][:, 2 * n * P : 2 * (n + 1) * P].bitcast(FP4X4),
+                    lhsT_scale=w4_s[a][:, n * P : (n + 1) * P],
+                    rhs=f_c[a][:, hf * HALF : (hf + 1) * HALF].bitcast(FP8X4),
+                    rhs_scale=f_s[a][:, hf * HALF : (hf + 1) * HALF],
                     start=(a == 0 and u == 0),
-                    stop=(a == 1 and u == per_bank - 1),
+                    stop=(a == 1 and u == 1),
                 )
 
-        y_sb = {(m0, g): sbuf("y%d_%d" % (m0, g), [P, PACK * w], F32) for m0, w in pieces for g in range(2)}
-        y_c = {(m0, g): sbuf("y_c%d_%d" % (m0, g), [P, w], U32) for m0, w in pieces for g in range(2)}
+        y_sb = {(hf, g): sbuf("y%d_%d" % (hf, g), [P, PACK, HALF], F32) for hf in range(2) for g in range(2)}
+        y_c = {(hf, g): sbuf("y_c%d_%d" % (hf, g), [P, HALF], U32) for hf in range(2) for g in range(2)}
         y_s = sbuf("y_s", [P, 2 * M], U8)
-        y_wv = {}
+        y_bf = {}
 
-        def y_out(m0, w, k, copy):
-            per_bank = BANK // w
-            g, t0 = divmod(k * per_bank, PACK)
-            part = y_sb[m0, g][:, t0 * w : (t0 + per_bank) * w]
-            copy(part, y_ps[m0, k][:])
-            rows = out_0[g * KP : (g + 1) * KP, m0 : m0 + w].rearrange("(p t) m -> p t m", t=PACK)
-            nc.sync.dma_start(rows[:, t0 : t0 + per_bank, :], part.rearrange("p (t m) -> p t m", m=w))
+        def y_out(hf, g):
+            rows = out_0[g * KP : (g + 1) * KP, hf * HALF : (hf + 1) * HALF].rearrange("(p t) m -> p t m", t=PACK)
+            for u in range(2):
+                part = y_sb[hf, g][:, 2 * u : 2 * u + 2, :]
+                nc.scalar.copy(part.rearrange("p t m -> p (t m)"), y_ps[hf, 2 * g + u][:])
+                if True:
+                    nc.sync.dma_start(rows[:, 2 * u : 2 * u + 2, :], part)
+            if not (True):
+                nc.sync.dma_start(rows, y_sb[hf, g][:])
 
-        def weave_y(m0, g, copy):
-            planar = y_sb[m0, g][:].rearrange("p (t m) -> p t m", t=PACK)
-            y_wv[m0, g] = weave("y_wv%d_%d" % (m0, g), planar, copy)
+        def weave_y(hf, g, copy):
+            y_bf[hf, g] = sbuf("y_bf%d_%d" % (hf, g), [P, PACK * HALF], BF16)
+            copy(woven(y_bf[hf, g]), planar(y_sb[hf, g][:]))
 
-        def quant_y(m0, w, g):
-            c0 = g * M + m0
-            nc.vector.quantize_mx(out=y_c[m0, g][:].bitcast(FP8X4), scales=y_s[:, c0 : c0 + w], in_=y_wv[m0, g][:])
+        def quant_y(hf, g):
+            c0 = g * M + hf * HALF
+            nc.vector.quantize_mx(out=y_c[hf, g][:].bitcast(FP8X4), scales=y_s[:, c0 : c0 + HALF], in_=y_bf[hf, g][:])
             words = out_1[g].rearrange("p m t -> p (m t)").bitcast(I32)
-            nc.sync.dma_start(words[:, m0 : m0 + w], y_c[m0, g][:].bitcast(I32))
-
-        on_s = nc.scalar.copy
-        on_v = nc.vector.tensor_copy
+            nc.sync.dma_start(words[:, hf * HALF : (hf + 1) * HALF], y_c[hf, g][:].bitcast(I32))
 
         nc.vector.tensor_copy(v_sc[:], tab_sc[:].indirect(offs_sb[:]))
-        gather_words(0)
-        gather_words(1)
+        for a in range(2):
+            nc.vector.tensor_copy(v_w[a][:], tab_w[a][:].indirect(offs_sb[:]))
         round_w1(0, 0, 0, on_s)
         round_w1(0, 0, 1, on_s)
         quant_w1(0, 0, 0)
@@ -297,65 +272,55 @@ def tile_list_limb_fluid_features_kernel(
         quant_w1(0, 1, 1)
 
         casts = [(0, on_v), (0, on_v), (1, on_v), (1, on_s)]
-        for i in range(8):
+        for i in range(TILES):
+            w = M if i < 4 else HALF
             h_out(i, 0, on_s)
             h_out(i, 1, on_v if i == 0 else on_s)
-            look(i, "all" if i < PACK else 0)
+            look(i, 0, w)
             pick(i)
-            if i > 0:
-                finish(i - 1, "all" if i - 1 < PACK else 0)
             for n, (at, eng) in enumerate(casts):
                 if at == i:
                     round_w1(1, n // 2, n % 2, eng)
-            join(i, "all" if i < PACK else 0)
+            add_look(i, 0, w)
             for n, (at, eng) in enumerate(casts):
                 if at == i:
                     quant_w1(1, n // 2, n % 2)
-            if i < 6:
+            if i + 2 < TILES:
                 h_pass(i + 2, 0)
                 h_pass(i + 2, 1)
+            if i == 4:
+                finish_f(0, 0, M)
+            if i == 5:
+                quant_f(0, 0, M)
             if i == 5:
                 deal_w4_scales()
             if i == 4:
                 deal_w4_words(0)
             if i == 5:
                 deal_w4_words(1)
-        weave_f(0, 0, HALF, on_s, None)
-        finish(7, 0)
-        quant_f(0, 0, HALF)
-        y_pass(0, HALF, 0)
-        weave_f(1, 0, HALF, on_v)
-        for i in range(4, 8):
-            look(i, 1)
-            if i > 4:
-                finish(i - 1, 1)
-            join(i, 1)
+        y_pass(0, 0)
+        y_pass(1, 0)
+        finish_f(1, 0, HALF)
+        for i in range(4, TILES):
+            look(i, HALF, HALF)
+            add_look(i, HALF, HALF)
             if i == 4:
                 quant_f(1, 0, HALF)
-                y_pass(0, HALF, 1)
-        weave_f(0, HALF, HALF, on_s, "a70")
-        for k in range(4):
-            y_out(0, HALF, k, on_s)
-        finish(7, 1)
-        quant_f(0, HALF, HALF)
-        y_pass(HALF, HALF, 0)
-        weave_f(1, HALF, HALF, on_v)
+                y_pass(0, 1)
+        y_out(0, 0)
+        y_out(0, 1)
+        finish_f(1, HALF, HALF)
         weave_y(0, 0, on_v)
         quant_f(1, HALF, HALF)
-        y_pass(HALF, HALF, 1)
+        y_pass(1, 1)
         weave_y(0, 1, on_v)
-        quant_y(0, HALF, 0)
-        quant_y(0, HALF, 1)
-        n = 0
-        for m0, w in pieces[1:]:
-            for k in range(2 * PACK * w // BANK):
-                y_out(m0, w, k, on_v if n in () else on_s)
-                n = n + 1
-        for m0, w in pieces[1:]:
-            for g in range(2):
-                weave_y(m0, g, on_v)
-            for g in range(2):
-                quant_y(m0, w, g)
+        quant_y(0, 0)
+        quant_y(0, 1)
+        for g in range(2):
+            y_out(1, g)
+        for g in range(2):
+            weave_y(1, g, on_v)
+            quant_y(1, g)
         for q in range(4):
             queue = nc.scalar if q % 2 else nc.sync
             queue.dma_start(

from contextlib import ExitStack

import concourse.mybir as mybir

K, H, N, T, S, M = 1024, 1024, 1024, 2048, 1024, 512
FLOPS = 2 * K * H * S + 2 * H * N * M

F32 = mybir.dt.float32
BF16 = mybir.dt.bfloat16
I32 = mybir.dt.int32
U32 = mybir.dt.uint32
U16 = mybir.dt.uint16
U8 = mybir.dt.uint8
FP8X4 = mybir.dt.float8_e4m3fn_x4
FP4X4 = mybir.dt.float4_e2m1fn_x4
MULT = mybir.AluOpType.mult
ADD = mybir.AluOpType.add
EXP = mybir.ActivationFunctionType.Exp
COPY = mybir.ActivationFunctionType.Copy

P = 128
PACK = 4
KP = P * PACK
BANK = 512
HALF = M // 2
TILES = H // P


def tile_list_limb_fluid_features_kernel(
    tc, tab_words, tab_scales, offs, pos1, pos2, w1, sc, sb, opp, gain, resid, w4_words, w4_scales, out_0, out_1, out_2
):
    nc = tc.nc
    with ExitStack() as ctx:
        keep = ctx.enter_context(tc.tile_pool(name="keep", bufs=1))
        psum = ctx.enter_context(tc.psum_pool(name="psum", bufs=1))

        def sbuf(name, shape, dtype):
            return keep.tile(shape, dtype, name=name, align_bytes=64)

        def bank(k, name):
            return psum.tile([P, BANK], F32, name=name, tag="bank%d" % k)

        on_s = nc.scalar.copy
        on_v = nc.vector.tensor_copy

        offs_sb = keep.tile([P, S // 16], U16, name="offs_sb")
        pos1_sb = keep.tile([P, M // 16], U16, name="pos1_sb")
        pos2_sb = keep.tile([P, M // 16], U16, name="pos2_sb")

        tab_sc = sbuf("tab_sc", [P, T], U8)
        nc.vector.memset(tab_sc[:].bitcast(I32), 0)
        w4_sc_raw = sbuf("w4_sc_raw", [P, N], U8)
        nc.gpsimd.memset(w4_sc_raw[:].bitcast(I32), 0)

        tab_w = [sbuf("tab_w%d" % a, [P, T], U32) for a in range(2)]
        w1_raw = {(b, a): sbuf("w1_raw%d%d" % (b, a), [P, PACK, KP], F32) for b in range(2) for a in range(2)}
        base = [sbuf("base%d" % b, [P, PACK, M], F32) for b in range(2)]
        w4_raw = sbuf("w4_raw", [P, 2, 2 * N], U8)

        def load_tab(a, c0, c1):
            words = tab_words[a].rearrange("p t i -> p (t i)").bitcast(I32)
            nc.sync.dma_start(tab_w[a][:, c0:c1].bitcast(I32), words[:, c0:c1])

        def load_w1(b, a):
            rows = w1[a * KP : (a + 1) * KP, b * KP : (b + 1) * KP]
            nc.sync.dma_start(w1_raw[b, a][:], rows.rearrange("(p j) c -> p j c", j=PACK))

        def load_resid(b, t0, t1):
            rows = resid[b * KP : (b + 1) * KP, :].rearrange("(p t) m -> p t m", t=PACK)
            nc.sync.dma_start(base[b][:, t0:t1, :], rows[:, t0:t1, :])

        def load_rows(name, vec, queue):
            tile = sbuf(name, [P, 16], F32)
            queue.dma_start(
                tile[:].rearrange("p (b u) -> p b u", b=2)[:, :, 0:PACK], vec.rearrange("(b p t) -> p b t", b=2, t=PACK)
            )
            return tile

        def load_planes(tile, scales):
            for q in range(4):
                nc.sync.dma_start(tile[32 * q : 32 * q + 8, :].bitcast(I32), scales[:, 4 * q : 4 * q + 4, :].bitcast(I32))

        opp_sb = load_rows("opp_sb", opp, nc.sync)
        gain_sb = load_rows("gain_sb", gain, nc.sync)
        nc.sync.dma_start(offs_sb[:], offs)
        load_tab(0, 0, T // 2)
        load_planes(tab_sc, tab_scales)
        load_tab(0, T // 2, T)
        load_tab(1, 0, T)
        load_w1(0, 0)
        load_w1(0, 1)
        nc.sync.dma_start(pos1_sb[:], pos1)
        nc.sync.dma_start(pos2_sb[:], pos2)
        sc_sb = load_rows("sc_sb", sc, nc.sync)
        sb_sb = load_rows("sb_sb", sb, nc.sync)
        load_resid(0, 0, 2)
        load_w1(1, 0)
        load_w1(1, 1)
        load_resid(0, 2, 4)
        nc.sync.dma_start(w4_raw[:].bitcast(I32), w4_words.rearrange("a p c -> p a c").bitcast(I32))
        load_planes(w4_sc_raw, w4_scales)
        load_resid(1, 0, 4)

        def col(tile, i):
            c = 8 * (i // PACK) + i % PACK
            return tile[:, c : c + 1]

        weight = [sbuf("weight%d" % i, [P, M], F32) for i in range(TILES)]
        for i in range(TILES):
            nc.scalar.activation(
                out=weight[i][:], in_=col(opp_sb, i).to_broadcast([P, M]), func=COPY, scale=col(gain_sb, i)
            )

        v_sc = sbuf("v_sc", [P, S], U8)
        v_w = [sbuf("v_w%d" % a, [P, S], U32) for a in range(2)]
        w1_bf = {}
        w1_c = {}
        w1_s = {}

        def round_w1(b, a, u, copy):
            tile = keep.tile([P, 2 * P * PACK], BF16, name="w1_bf", bufs=4, align_bytes=64)
            src = w1_raw[b, a][:].rearrange("p j (m t) -> p m j t", t=PACK)[:, :, :, 2 * u : 2 * u + 2]
            copy(tile[:].rearrange("p (t m j) -> p m j t", t=2, j=PACK), src)
            w1_bf[b, a, u] = tile

        def quant_w1(b, a, u):
            w1_c[b, a, u] = sbuf("w1_c%d%d%d" % (b, a, u), [P, 2 * P], U32)
            w1_s[b, a, u] = sbuf("w1_s%d%d%d" % (b, a, u), [P, 2 * P], U8)
            nc.vector.quantize_mx(out=w1_c[b, a, u][:].bitcast(FP8X4), scales=w1_s[b, a, u][:], in_=w1_bf[b, a, u][:])

        h_ps = {}

        def h_pass(i, a):
            b, t = divmod(i, PACK)
            cols = slice((t % 2) * P, (t % 2 + 1) * P)
            for c in range(2):
                if a == 0:
                    h_ps[i, c] = bank(2 * (i % 2) + c, "h_ps%d%d" % (i, c))
                sl = slice(c * BANK, (c + 1) * BANK)
                nc.tensor.matmul_mx(
                    out=h_ps[i, c][:],
                    lhsT=w1_c[b, a, t // 2][:, cols].bitcast(FP8X4),
                    lhsT_scale=w1_s[b, a, t // 2][:, cols],
                    rhs=v_w[a][:, sl].bitcast(FP8X4),
                    rhs_scale=v_sc[4 * a : P, sl],
                    start=(a == 0),
                    stop=(a == 1),
                )

        h_sb = [sbuf("h%d" % i, [P, S], F32) for i in range(TILES)]
        picked = [sbuf("picked%d" % b, [P, PACK, M], F32) for b in range(2)]
        looked = {}

        def h_out(i, c, copy):
            copy(h_sb[i][:, c * BANK : (c + 1) * BANK], h_ps[i, c][:])

        def look(i, m0, w):
            looked[i, m0] = sbuf("looked%d_%d" % (i, m0), [P, w], F32)
            nc.scalar.activation(
                out=looked[i, m0][:],
                in_=h_sb[i][:].indirect(pos1_sb[:, m0 // 16 : (m0 + w) // 16]),
                func=EXP,
                bias=col(sb_sb, i),
                scale=col(sc_sb, i),
            )

        def pick(i):
            b, t = divmod(i, PACK)
            nc.vector.tensor_tensor(picked[b][:, t, :], h_sb[i][:].indirect(pos2_sb[:]), weight[i][:], MULT)

        def add_look(i, m0, w):
            b, t = divmod(i, PACK)
            part = base[b][:, t, m0 : m0 + w]
            nc.vector.scalar_tensor_tensor(part, looked[i, m0][:], col(gain_sb, i), part, MULT, ADD)

        def woven(tile):
            return tile[:].rearrange("p (c i t) -> p c t i", i=2, t=PACK)

        def planar(rows):
            return rows.rearrange("p t (c i) -> p c t i", i=2)

        f_bf = {}
        f_c = [sbuf("f_c%d" % b, [P, M], U32) for b in range(2)]
        f_s = [sbuf("f_s%d" % b, [P, M], U8) for b in range(2)]

        def finish_f(b, m0, w):
            f_bf[b, m0] = sbuf("f_bf%d_%d" % (b, m0), [P, PACK * w], BF16)
            nc.vector.tensor_tensor(
                woven(f_bf[b, m0]), planar(picked[b][:, :, m0 : m0 + w]), planar(base[b][:, :, m0 : m0 + w]), ADD
            )

        def quant_f(b, m0, w):
            nc.vector.quantize_mx(
                out=f_c[b][:, m0 : m0 + w].bitcast(FP8X4), scales=f_s[b][:, m0 : m0 + w], in_=f_bf[b, m0][:]
            )

        w4_w = [sbuf("w4_w%d" % a, [P, 2 * N], U8) for a in range(2)]
        w4_s = [sbuf("w4_s%d" % a, [P, N], U8) for a in range(2)]

        def deal_w4_words(a):
            nc.scalar.copy(
                w4_w[a][:].bitcast(U16).rearrange("p (g t m) -> p g t m", t=PACK, m=P),
                w4_raw[:, a, :].bitcast(U16).rearrange("p (g m t) -> p g t m", t=PACK, m=P),
            )

        def deal_w4_scales():
            nc.vector.tensor_copy(
                w4_s[0][:].rearrange("p (g t m) -> p g t m", t=PACK, m=P),
                w4_sc_raw[:].rearrange("p (g m t) -> p g t m", t=PACK, m=P),
            )
            for q in range(4):
                nc.sync.dma_start(
                    w4_s[1][32 * q : 32 * q + 4, :].bitcast(I32), w4_s[0][32 * q + 4 : 32 * q + 8, :].bitcast(I32)
                )

        y_ps = {}

        def y_pass(hf, a):
            for n in range(2 * PACK):
                k, u = divmod(n, 2)
                if a == 0 and u == 0:
                    y_ps[hf, k] = bank(4 * (1 - hf) + k, "y_ps%d_%d" % (hf, k))
                nc.tensor.matmul_mx(
                    out=y_ps[hf, k][:, u * HALF : (u + 1) * HALF],
                    lhsT=w4_w[a][:, 2 * n * P : 2 * (n + 1) * P].bitcast(FP4X4),
                    lhsT_scale=w4_s[a][:, n * P : (n + 1) * P],
                    rhs=f_c[a][:, hf * HALF : (hf + 1) * HALF].bitcast(FP8X4),
                    rhs_scale=f_s[a][:, hf * HALF : (hf + 1) * HALF],
                    start=(a == 0 and u == 0),
                    stop=(a == 1 and u == 1),
                )

        y_sb = {(hf, g): sbuf("y%d_%d" % (hf, g), [P, PACK, HALF], F32) for hf in range(2) for g in range(2)}
        y_c = {(hf, g): sbuf("y_c%d_%d" % (hf, g), [P, HALF], U32) for hf in range(2) for g in range(2)}
        y_s = sbuf("y_s", [P, 2 * M], U8)
        y_bf = {}

        def y_out(hf, g):
            rows = out_0[g * KP : (g + 1) * KP, hf * HALF : (hf + 1) * HALF].rearrange("(p t) m -> p t m", t=PACK)
            for u in range(2):
                part = y_sb[hf, g][:, 2 * u : 2 * u + 2, :]
                nc.scalar.copy(part.rearrange("p t m -> p (t m)"), y_ps[hf, 2 * g + u][:])
                if True:
                    nc.sync.dma_start(rows[:, 2 * u : 2 * u + 2, :], part)
            if not (True):
                nc.sync.dma_start(rows, y_sb[hf, g][:])

        def weave_y(hf, g, copy):
            y_bf[hf, g] = sbuf("y_bf%d_%d" % (hf, g), [P, PACK * HALF], BF16)
            copy(woven(y_bf[hf, g]), planar(y_sb[hf, g][:]))

        def quant_y(hf, g):
            c0 = g * M + hf * HALF
            nc.vector.quantize_mx(out=y_c[hf, g][:].bitcast(FP8X4), scales=y_s[:, c0 : c0 + HALF], in_=y_bf[hf, g][:])
            words = out_1[g].rearrange("p m t -> p (m t)").bitcast(I32)
            nc.sync.dma_start(words[:, hf * HALF : (hf + 1) * HALF], y_c[hf, g][:].bitcast(I32))

        nc.vector.tensor_copy(v_sc[:], tab_sc[:].indirect(offs_sb[:]))
        for a in range(2):
            nc.vector.tensor_copy(v_w[a][:], tab_w[a][:].indirect(offs_sb[:]))
        round_w1(0, 0, 0, on_s)
        round_w1(0, 0, 1, on_s)
        quant_w1(0, 0, 0)
        h_pass(0, 0)
        h_pass(1, 0)
        round_w1(0, 1, 0, on_v)
        round_w1(0, 1, 1, on_s)
        quant_w1(0, 0, 1)
        quant_w1(0, 1, 0)
        h_pass(0, 1)
        h_pass(1, 1)
        quant_w1(0, 1, 1)

        casts = [(0, on_v), (0, on_v), (1, on_v), (1, on_s)]
        for i in range(TILES):
            w = M if i < 4 else HALF
            h_out(i, 0, on_s)
            h_out(i, 1, on_v if i == 0 else on_s)
            look(i, 0, w)
            pick(i)
            for n, (at, eng) in enumerate(casts):
                if at == i:
                    round_w1(1, n // 2, n % 2, eng)
            add_look(i, 0, w)
            for n, (at, eng) in enumerate(casts):
                if at == i:
                    quant_w1(1, n // 2, n % 2)
            if i + 2 < TILES:
                h_pass(i + 2, 0)
                h_pass(i + 2, 1)
            if i == 4:
                finish_f(0, 0, M)
            if i == 5:
                quant_f(0, 0, M)
            if i == 5:
                deal_w4_scales()
            if i == 4:
                deal_w4_words(0)
            if i == 5:
                deal_w4_words(1)
        y_pass(0, 0)
        y_pass(1, 0)
        finish_f(1, 0, HALF)
        for i in range(4, TILES):
            look(i, HALF, HALF)
            add_look(i, HALF, HALF)
            if i == 4:
                quant_f(1, 0, HALF)
                y_pass(0, 1)
        y_out(0, 0)
        y_out(0, 1)
        finish_f(1, HALF, HALF)
        weave_y(0, 0, on_v)
        quant_f(1, HALF, HALF)
        y_pass(1, 1)
        weave_y(0, 1, on_v)
        quant_y(0, 0)
        quant_y(0, 1)
        for g in range(2):
            y_out(1, g)
        for g in range(2):
            weave_y(1, g, on_v)
            quant_y(1, g)
        for q in range(4):
            queue = nc.scalar if q % 2 else nc.sync
            queue.dma_start(
                out_2[:, 4 * q : 4 * q + 4, :].rearrange("g r m -> r g m").bitcast(I32),
                y_s[32 * q : 32 * q + 4, :].rearrange("r (g m) -> r g m", g=2).bitcast(I32),
            )
